import numpy as np
import ml_dtypes


def mxq(x, axis, fmt="e4m3"):
    dtype, down = {"e4m3": (ml_dtypes.float8_e4m3fn, 7), "e5m2": (ml_dtypes.float8_e5m2, 14)}[fmt]
    v = np.moveaxis(np.asarray(x, np.float32).astype(ml_dtypes.bfloat16).astype(np.float64), axis, -1)
    blocks = v.reshape(v.shape[:-1] + (-1, 32))
    amax = np.abs(blocks).max(-1, keepdims=True)
    byte = np.maximum(np.where(amax > 0, np.frexp(amax)[1] - 1 + 127, 0) - down, 1)
    scale = np.exp2(byte - 127.0)
    codes = (blocks / scale).astype(np.float32).astype(dtype).astype(np.float64)
    return np.moveaxis((codes * scale).reshape(v.shape), -1, axis)


WIDE = False


def mx_kscale(k):
    if not WIDE:
        return np.ones(k)
    levels = np.array([10, -10, 5, -5, 0])
    if k % 512:
        return np.exp2(np.random.permutation(np.resize(levels, k // 32))).repeat(32)
    a = np.empty((k // 512, 16))
    for p in range(k // 512):
        a[p, :8] = np.random.permutation(np.resize(levels, 8))
        for g in range(8):
            far = levels[np.abs(levels - a[p, g]) >= 10]
            a[p, g + 8] = far[np.random.randint(len(far))]
    return np.exp2(a.ravel()).repeat(32)


def f64(x):
    return np.asarray(x).astype(np.float64)


def striped(idx):
    return np.tile(idx.reshape(-1, 16).T, (8, 1)).astype(np.uint16)


def unstriped(offs):
    return offs[:16].T.reshape(-1).astype(np.int64)


def striped8(idx):
    return np.concatenate([x.reshape(-1, 16).T for x in idx]).astype(np.uint16)


def runs(offs, k):
    lists = np.stack([offs[16 * r : 16 * r + 16].T.reshape(-1) for r in range(8)]).astype(np.int64)
    return lists[np.arange(k) % 512 // 64]


def pack_weight(w):
    k, n = w.shape
    w = f64(np.asarray(w, np.float32).astype(ml_dtypes.bfloat16)).reshape(k // 32, 32, n)
    amax = np.abs(w).max(1)
    byte = np.clip(np.where(amax > 0, np.frexp(amax)[1] - 1 + 127 - 7, 1), 1, 254)
    scaled = (w * np.exp2(127.0 - byte)[:, None, :]).reshape(k, n).astype(np.float32)
    words = np.ascontiguousarray(scaled.reshape(k // 512, 128, 4, n).transpose(0, 1, 3, 2)).astype(ml_dtypes.float8_e4m3fn).view(np.uint8)
    return words, np.ascontiguousarray(byte.astype(np.uint8).reshape(k // 512, 16, n))


def unpack_weight(words, scales):
    g, p, n, _ = words.shape
    vals = np.ascontiguousarray(words).view(ml_dtypes.float8_e4m3fn).astype(np.float64) * np.repeat(np.exp2(scales.astype(np.float64) - 127.0), 8, axis=1)[..., None]
    return vals.transpose(0, 1, 3, 2).reshape(g * 512, n)


K, T, S, N, H, W = 512, 2048, 512, 512, 512, 2048


def setup_inputs():
    n = np.random.standard_normal
    s = mx_kscale(K)[:, None]
    u = mx_kscale(H)
    packed_xT = pack_weight(n((K, T)) * s)
    return {
        "x_words": packed_xT[0],
        "x_scales": packed_xT[1],
        "w1": (n((K, H)) / np.sqrt(K) / s).astype(np.float32),
        "gn": (np.random.uniform(0.5, 1.5, (H, 1)) * u[:, None]).astype(np.float32),
        "w2": (n((H, N)) / np.sqrt(2 * H) / u[:, None]).astype(np.float32),
        "w3": (n((K, N)) / np.sqrt(2 * K) / s).astype(np.float32),
        "offs": striped(np.random.permutation(T)[:S]),
        "n1": striped(np.random.randint(0, S, W)),
        "hz": striped8(np.random.randint(0, T, (8, S))),
        "n2": striped8(np.stack([np.random.permutation(S) for _ in range(8)])),
        "n3": striped8(np.stack([np.random.permutation(S) for _ in range(8)])),
    }


def reference(x_words, x_scales, w1, gn, w2, w3, offs, n1, hz, n2, n3):
    xq = unpack_weight(x_words, x_scales)[:, unstriped(offs)]
    y = mxq(f64(w1), 0, "e4m3").T @ xq
    mb = y[:, unstriped(n1)]
    mx = mb.reshape(H, S, 4).max(axis=2)
    mn = mb.reshape(H, S, 4).min(axis=2)
    z = f64(gn) * (mx - (0.5 * mn))
    x_hz = unpack_weight(x_words, x_scales)[np.arange(K)[:, None], runs(hz, K)]
    h = mxq(f64(w2), 0, "e4m3").T @ mxq(z, 0, "e4m3") + mxq(f64(w3), 0, "e4m3").T @ x_hz
    return (h - (h[np.arange(N)[:, None], runs(n2, N)])) / (np.abs(h[np.arange(N)[:, None], runs(n3, N)] - h) + 0.5)

@@ -1,0 +1,295 @@
+from contextlib import ExitStack
+
+import concourse.mybir as mybir
+
+F32 = mybir.dt.float32
+BF16 = mybir.dt.bfloat16
+I32 = mybir.dt.int32
+U32 = mybir.dt.uint32
+U16 = mybir.dt.uint16
+U8 = mybir.dt.uint8
+FP8X4 = mybir.dt.float8_e4m3fn_x4
+ALU = mybir.AluOpType
+ACT = mybir.ActivationFunctionType
+
+P = 128
+PACK = 4
+T = 2048
+S = 512
+MEMBERS = 4
+CHUNK = 128
+CHUNKS = S // CHUNK
+SPARE = 32
+
+FLOPS = 3 * 2 * 512 * 512 * 512
+
+
+def tile_picked_mixhgspanfrac_none_p_kernel(
+    tc, x_words, x_scales, w1, gn, w2, w3, offs, n1, hz, n2, n3, out
+):
+    nc = tc.nc
+    with ExitStack() as ctx:
+        keep = ctx.enter_context(tc.tile_pool(name="keep", bufs=1))
+        ring = ctx.enter_context(tc.tile_pool(name="ring", bufs=2))
+        psum = ctx.enter_context(tc.psum_pool(name="psum", bufs=1))
+
+        def load_list(src, name):
+            lst = keep.tile(list(src.shape), U16, name=name)
+            nc.sync.dma_start(lst[:], src)
+            return lst
+
+        def load_weight(w, name, c0, c1):
+            raw = keep.tile([P, PACK, c1 - c0], F32, name=name)
+            nc.sync.dma_start(raw[:], w.rearrange("(p j) c -> p j c", j=PACK)[:, :, c0:c1])
+            return raw
+
+        def deal(copy, grouped, raw, m0, m1):
+            copy(
+                grouped[:].rearrange("p (t m j) -> p m j t", t=PACK, j=PACK)[:, m0:m1],
+                raw[:].rearrange("p j (m t) -> p m j t", t=PACK),
+            )
+
+        def mx_tiles(name, width):
+            codes = keep.tile([P, width], U32, name=name + "_codes", align_bytes=64)
+            scales = keep.tile([P, width], U8, name=name + "_scales", align_bytes=64)
+            return codes, scales
+
+        xs = keep.tile([P, T], U8, name="xs", align_bytes=64)
+        nc.vector.memset(xs[:].bitcast(I32), 0)
+        xs_runs = keep.tile([P, T], U8, name="xs_runs", align_bytes=64)
+        nc.gpsimd.memset(xs_runs[:].bitcast(I32), 0)
+        scale_rows = x_scales[0].bitcast(I32)
+        offs_t = load_list(offs, "offs_t")
+        hz_t = load_list(hz, "hz_t")
+        n1_t = load_list(n1, "n1_t")
+        n2_t = load_list(n2, "n2_t")
+        n3_t = load_list(n3, "n3_t")
+        gain = keep.tile([P, PACK], F32, name="gain")
+        nc.sync.dma_start(gain[:], gn.rearrange("(p t) o -> p (t o)", t=PACK))
+        xw = keep.tile([P, T], U32, name="xw", align_bytes=64)
+        nc.sync.dma_start(xw[:].bitcast(I32), x_words[0].rearrange("p n t -> p (n t)").bitcast(I32))
+        for b in range(4):
+            nc.sync.dma_start(xs[:].bitcast(I32)[b:P:32, :], scale_rows[b:16:4, :])
+        w1_raw = [load_weight(w1, "w1_raw%d" % h, 256 * h, 256 * (h + 1)) for h in range(2)]
+        nc.sync.dma_start(xs_runs[:].bitcast(I32)[0:P:8, :], scale_rows)
+        w3_raw = load_weight(w3, "w3_raw", 0, 512)
+        w2_raw = load_weight(w2, "w2_raw", 0, 512)
+
+        y_win = [keep.tile([P, S + SPARE], F32, name="y_win%d" % t) for t in range(PACK)]
+        for t in range(PACK):
+            nc.gpsimd.memset(y_win[t][:, S:], 0.0)
+        xh_plane = keep.tile([P, S], U8, name="xh_plane", align_bytes=64)
+        nc.gpsimd.memset(xh_plane[:].bitcast(I32), 0)
+        h_win = [keep.tile([P, 2 * S], F32, name="h_win%d" % t) for t in range(PACK)]
+        for t in range(PACK):
+            nc.gpsimd.memset(h_win[t][:, S:], 0.0)
+
+        step = keep.tile([P, PACK], F32, name="step")
+        nc.vector.tensor_scalar(step[:], gain[:], 0.0, 2.0, ALU.is_ge, ALU.mult)
+        sign = keep.tile([P, PACK], F32, name="sign")
+        nc.vector.tensor_scalar(sign[:], step[:], 1.0, None, ALU.subtract)
+        size = keep.tile([P, PACK], F32, name="size")
+        nc.vector.tensor_tensor(size[:], gain[:], sign[:], ALU.mult)
+
+        xq_codes, xq_scales = mx_tiles("xq", S)
+        xh_codes, xh_bytes = mx_tiles("xh", S)
+        w1_grouped = keep.tile([P, PACK * 512], BF16, name="w1_grouped", align_bytes=64)
+        w1_codes, w1_scales = mx_tiles("w1", 512)
+        deal(nc.scalar.copy, w1_grouped, w1_raw[0], 0, 64)
+        deal(nc.vector.tensor_copy, w1_grouped, w1_raw[1], 64, 128)
+        nc.vector.tensor_copy(xq_codes[:], xw[:].indirect(offs_t[:]))
+        nc.vector.tensor_copy(xq_scales[:], xs[:].indirect(offs_t[:]))
+        for u in range(2):
+            cols = slice(256 * u, 256 * (u + 1))
+            nc.vector.quantize_mx(
+                out=w1_codes[:, cols].bitcast(FP8X4),
+                scales=w1_scales[:, cols],
+                in_=w1_grouped[:, 1024 * u : 1024 * (u + 1)],
+            )
+        nc.vector.tensor_copy(xh_bytes[:], xs_runs[:].indirect(hz_t[:]))
+        for b in range(4):
+            nc.sync.dma_start(xh_plane[:].bitcast(I32)[b:P:32, :], xh_bytes[:].bitcast(I32)[8 * b : P : 32, :])
+        for t in range(PACK):
+            y_ps = psum.tile([P, S], F32, name="y_ps%d" % t)
+            cols = slice(P * t, P * (t + 1))
+            nc.tensor.matmul_mx(
+                out=y_ps[:],
+                lhsT=w1_codes[:, cols].bitcast(FP8X4),
+                lhsT_scale=w1_scales[:, cols],
+                rhs=xq_codes[:].bitcast(FP8X4),
+                rhs_scale=xq_scales[:],
+                start=True,
+                stop=True,
+            )
+            if t % 2:
+                nc.vector.tensor_scalar(y_win[t][:, :S], y_ps[:], size[:, t : t + 1], None, ALU.mult)
+            else:
+                nc.scalar.activation(y_win[t][:, :S], y_ps[:], ACT.Copy, scale=size[:, t : t + 1])
+
+        nc.vector.tensor_copy(xh_codes[:], xw[:].indirect(hz_t[:]))
+        w_mx = {}
+        for name, raw in (("w3", w3_raw), ("w2", w2_raw)):
+            grouped = keep.tile([P, PACK * 512], BF16, name=name + "_grouped", align_bytes=64)
+            if name == "w3":
+                deal(nc.vector.tensor_copy, grouped, raw, 0, P)
+            else:
+                signs = sign[:].unsqueeze(1).unsqueeze(3).to_broadcast([P, P, PACK, PACK])
+                deal(lambda o, i: nc.vector.tensor_tensor(o, i, signs, ALU.mult), grouped, raw, 0, P)
+            w_mx[name] = (grouped,) + mx_tiles(name, 512)
+        for name in ("w3", "w2"):
+            grouped, codes, scales = w_mx[name]
+            nc.vector.quantize_mx(out=codes[:].bitcast(FP8X4), scales=scales[:], in_=grouped[:])
+        w3_codes, w3_scales = w_mx["w3"][1:]
+        w2_codes, w2_scales = w_mx["w2"][1:]
+
+        h_ps = [psum.tile([P, PACK, CHUNK], F32, name="h_ps%d" % c) for c in range(CHUNKS)]
+        h_plain = keep.tile([P, PACK, S], F32, name="h_plain")
+
+        def hashed_product(c):
+            cols = slice(CHUNK * c, CHUNK * (c + 1))
+            for t in range(PACK):
+                rows = slice(P * t, P * (t + 1))
+                nc.tensor.matmul_mx(
+                    out=h_ps[c][:, t, :],
+                    lhsT=w3_codes[:, rows].bitcast(FP8X4),
+                    lhsT_scale=w3_scales[:, rows],
+                    rhs=xh_codes[:, cols].bitcast(FP8X4),
+                    rhs_scale=xh_plane[:, cols],
+                    start=(t == 0),
+                    stop=False,
+                )
+
+        state = {}
+        z_mx = [mx_tiles("z%d" % c, CHUNK) for c in range(CHUNKS)]
+        pieces = [(CHUNK * c, CHUNK) for c in range(CHUNKS - 1)] + [(S - CHUNK, CHUNK // 2), (S - CHUNK // 2, CHUNK // 2)]
+
+        def gather_members(k):
+            j0, n = pieces[k]
+            g = ring.tile([P, PACK, MEMBERS * n], F32, name="members", bufs=3)
+            lst = n1_t[:, j0 // 4 : (j0 + n) // 4]
+            for t in range(PACK):
+                if (k, t) == (0, 1):
+                    nc.vector.tensor_copy(g[:, t, :], y_win[t][:].indirect(lst))
+                else:
+                    nc.scalar.activation(g[:, t, :], y_win[t][:].indirect(lst), ACT.Copy)
+            state["g", k] = g
+
+        def pairs(k, op, name):
+            g = state["g", k][:].rearrange("p t (j h e) -> p j t h e", h=2, e=2)
+            r = ring.tile([P, pieces[k][1], PACK, 2], F32, name=name)
+            nc.vector.tensor_tensor(r[:], g[:, :, :, 0, :], g[:, :, :, 1, :], op)
+            state[name, k] = r
+
+        def fours(k, op, src, name):
+            r = ring.tile([P, pieces[k][1], PACK], F32, name=name)
+            nc.vector.tensor_tensor(r[:], state[src, k][:, :, :, 0], state[src, k][:, :, :, 1], op)
+            state[name, k] = r
+
+        def span(k):
+            z = ring.tile([P, pieces[k][1] * PACK], BF16, name="z", align_bytes=64)
+            flat = lambda name: state[name, k][:].rearrange("p j t -> p (j t)")
+            nc.vector.scalar_tensor_tensor(z[:], flat("mn"), -0.5, flat("mx"), ALU.mult, ALU.add)
+            state["z", k] = z
+
+        def second_product(k):
+            j0, n = pieces[k]
+            c = j0 // CHUNK
+            z_codes, z_scales = z_mx[c]
+            x = slice(j0 % CHUNK, j0 % CHUNK + n)
+            nc.vector.quantize_mx(out=z_codes[:, x].bitcast(FP8X4), scales=z_scales[:, x], in_=state["z", k][:])
+            if (j0 + n) % CHUNK:
+                return
+            for t in range(PACK):
+                rows = slice(P * t, P * (t + 1))
+                nc.tensor.matmul_mx(
+                    out=h_ps[c][:, t, :],
+                    lhsT=w2_codes[:, rows].bitcast(FP8X4),
+                    lhsT_scale=w2_scales[:, rows],
+                    rhs=z_codes[:].bitcast(FP8X4),
+                    rhs_scale=z_scales[:],
+                    start=False,
+                    stop=(t == PACK - 1),
+                )
+            empty_h(c)
+
+        def empty_h(c):
+            cols = slice(CHUNK * c, CHUNK * (c + 1))
+            nc.scalar.copy(h_plain[:, :, cols], h_ps[c][:])
+            for t in range(PACK):
+                if c == CHUNKS - 1 and t < 2:
+                    nc.vector.tensor_copy(h_win[t][:, cols], h_plain[:, t, cols])
+                else:
+                    nc.sync.dma_start(h_win[t][:, cols], h_plain[:, t, cols])
+
+        for c in range(CHUNKS):
+            hashed_product(c)
+        for k in range(len(pieces) + 1):
+            more = k < len(pieces)
+            if more:
+                gather_members(k)
+                pairs(k, ALU.max, "mx2")
+            if k > 0:
+                span(k - 1)
+            if more:
+                pairs(k, ALU.min, "mn2")
+            if k > 0:
+                second_product(k - 1)
+            if more:
+                fours(k, ALU.max, "mx2", "mx")
+                fours(k, ALU.min, "mn2", "mn")
+
+        out_rows = out.rearrange("(p t) c -> p t c", t=PACK)
+        parts = {}
+
+        def fetch(t):
+            a = keep.tile([P, S], F32, name="fetched%d" % t)
+            nc.scalar.activation(a[:], h_win[t][:].indirect(n2_t[:]), ACT.Copy)
+            parts["a", t] = a
+
+        def distance(t):
+            d = keep.tile([P, S], F32, name="d3_%d" % t)
+            nc.vector.tensor_tensor(d[:], h_win[t][:].indirect(n3_t[:]), h_plain[:, t, :], ALU.subtract)
+            parts["d", t] = d
+
+        def inverse(t):
+            a = ring.tile([P, S], F32, name="absd")
+            nc.scalar.activation(a[:], parts["d", t][:], ACT.Abs)
+            r = ring.tile([P, S], F32, name="root")
+            nc.scalar.activation(r[:], a[:], ACT.Abs_reciprocal_sqrt, bias=0.5)
+            q = keep.tile([P, S], F32, name="inv%d" % t)
+            nc.scalar.activation(q[:], r[:], ACT.Square)
+            parts["q", t] = q
+
+        def numerator(t):
+            n = keep.tile([P, S], F32, name="d2_%d" % t)
+            if ("a", t) in parts:
+                nc.vector.tensor_tensor(n[:], parts["a", t][:], h_plain[:, t, :], ALU.subtract)
+            else:
+                nc.vector.tensor_tensor(n[:], h_win[t][:].indirect(n2_t[:]), h_plain[:, t, :], ALU.subtract)
+            parts["n", t] = n
+
+        def quotient(t, pieces):
+            o = keep.tile([P, S], F32, name="o%d" % t)
+            for k in range(pieces):
+                x = slice(S // pieces * k, S // pieces * (k + 1))
+                nc.vector.scalar_tensor_tensor(o[:, x], parts["n", t][:, x], -1.0, parts["q", t][:, x], ALU.mult, ALU.mult)
+                nc.sync.dma_start(out_rows[:, t, x], o[:, x])
+
+        fetch(0)
+        distance(0)
+        inverse(0)
+        distance(1)
+        inverse(1)
+        numerator(0)
+        distance(2)
+        quotient(0, 1)
+        fetch(1)
+        distance(3)
+        inverse(2)
+        numerator(2)
+        numerator(1)
+        quotient(1, 1)
+        inverse(3)
+        numerator(3)
+        quotient(2, 1)
+        quotient(3, 2)

@@ -39,7 +39,7 @@ def tile_picked_mixhgspanfrac_none_p_kernel(
             return lst
 
         def load_weight(w, name, c0, c1):
-            raw = keep.tile([P, PACK, c1 - c0], F32, name=name)
+            raw = keep.tile([P, PACK, c1 - c0], F32, name=name, tag=name, align_bytes=64)
             nc.sync.dma_start(raw[:], w.rearrange("(p j) c -> p j c", j=PACK)[:, :, c0:c1])
             return raw
 
@@ -54,10 +54,13 @@ def tile_picked_mixhgspanfrac_none_p_kernel(
             scales = keep.tile([P, width], U8, name=name + "_scales", align_bytes=64)
             return codes, scales
 
+        warm = keep.tile([P, 2], F32, name="warm")
+        nc.vector.memset(warm[:, 0:1], 1.0)
+        nc.scalar.activation(warm[:, 1:2], warm[:, 0:1], ACT.Abs_reciprocal_sqrt)
         xs = keep.tile([P, T], U8, name="xs", align_bytes=64)
         nc.vector.memset(xs[:].bitcast(I32), 0)
         xs_runs = keep.tile([P, T], U8, name="xs_runs", align_bytes=64)
-        nc.gpsimd.memset(xs_runs[:].bitcast(I32), 0)
+        nc.vector.memset(xs_runs[:].bitcast(I32), 0)
         scale_rows = x_scales[0].bitcast(I32)
         offs_t = load_list(offs, "offs_t")
         hz_t = load_list(hz, "hz_t")
@@ -77,12 +80,12 @@ def tile_picked_mixhgspanfrac_none_p_kernel(
 
         y_win = [keep.tile([P, S + SPARE], F32, name="y_win%d" % t) for t in range(PACK)]
         for t in range(PACK):
-            nc.gpsimd.memset(y_win[t][:, S:], 0.0)
+            nc.vector.memset(y_win[t][:, S:], 0.0)
         xh_plane = keep.tile([P, S], U8, name="xh_plane", align_bytes=64)
-        nc.gpsimd.memset(xh_plane[:].bitcast(I32), 0)
+        nc.vector.memset(xh_plane[:].bitcast(I32), 0)
         h_win = [keep.tile([P, 2 * S], F32, name="h_win%d" % t) for t in range(PACK)]
         for t in range(PACK):
-            nc.gpsimd.memset(h_win[t][:, S:], 0.0)
+            nc.vector.memset(h_win[t][:, S:], 0.0)
 
         step = keep.tile([P, PACK], F32, name="step")
         nc.vector.tensor_scalar(step[:], gain[:], 0.0, 2.0, ALU.is_ge, ALU.mult)
@@ -92,8 +95,7 @@ def tile_picked_mixhgspanfrac_none_p_kernel(
         nc.vector.tensor_tensor(size[:], gain[:], sign[:], ALU.mult)
 
         xq_codes, xq_scales = mx_tiles("xq", S)
-        xh_codes, xh_bytes = mx_tiles("xh", S)
-        w1_grouped = keep.tile([P, PACK * 512], BF16, name="w1_grouped", align_bytes=64)
+        w1_grouped = keep.tile([P, PACK * 512], BF16, name="w1_grouped", tag="w1_grouped", align_bytes=64)
         w1_codes, w1_scales = mx_tiles("w1", 512)
         deal(nc.scalar.copy, w1_grouped, w1_raw[0], 0, 64)
         deal(nc.vector.tensor_copy, w1_grouped, w1_raw[1], 64, 128)
@@ -106,11 +108,13 @@ def tile_picked_mixhgspanfrac_none_p_kernel(
                 scales=w1_scales[:, cols],
                 in_=w1_grouped[:, 1024 * u : 1024 * (u + 1)],
             )
+        xh_bytes = keep.tile([P, S], U8, name="xh_bytes", tag="w1_raw1", align_bytes=64)
+        xh_codes = keep.tile([P, S], U32, name="xh_codes", tag="w1_grouped", align_bytes=64)
         nc.vector.tensor_copy(xh_bytes[:], xs_runs[:].indirect(hz_t[:]))
         for b in range(4):
             nc.sync.dma_start(xh_plane[:].bitcast(I32)[b:P:32, :], xh_bytes[:].bitcast(I32)[8 * b : P : 32, :])
         for t in range(PACK):
-            y_ps = psum.tile([P, S], F32, name="y_ps%d" % t)
+            y_ps = psum.tile([P, S], F32, name="y_ps%d" % t, tag="y_ps%d" % t)
             cols = slice(P * t, P * (t + 1))
             nc.tensor.matmul_mx(
                 out=y_ps[:],
@@ -142,7 +146,14 @@ def tile_picked_mixhgspanfrac_none_p_kernel(
         w3_codes, w3_scales = w_mx["w3"][1:]
         w2_codes, w2_scales = w_mx["w2"][1:]
 
-        h_ps = [psum.tile([P, PACK, CHUNK], F32, name="h_ps%d" % c) for c in range(CHUNKS)]
+        h_ps = [psum.tile([P, PACK, CHUNK], F32, name="h_ps%d" % c) for c in range(CHUNKS - 1)]
+        h_last = [psum.tile([P, 2, CHUNK], F32, name="h_last%d" % u, tag="y_ps%d" % u) for u in range(2)]
+
+        def h_sum(c, t):
+            if c < CHUNKS - 1:
+                return h_ps[c][:, t, :], t == 0, t == PACK - 1
+            return h_last[t // 2][:, t % 2, :], t % 2 == 0, t % 2 == 1
+
         h_plain = keep.tile([P, PACK, S], F32, name="h_plain")
 
         def hashed_product(c):
@@ -150,12 +161,12 @@ def tile_picked_mixhgspanfrac_none_p_kernel(
             for t in range(PACK):
                 rows = slice(P * t, P * (t + 1))
                 nc.tensor.matmul_mx(
-                    out=h_ps[c][:, t, :],
+                    out=h_sum(c, t)[0],
                     lhsT=w3_codes[:, rows].bitcast(FP8X4),
                     lhsT_scale=w3_scales[:, rows],
                     rhs=xh_codes[:, cols].bitcast(FP8X4),
                     rhs_scale=xh_plane[:, cols],
-                    start=(t == 0),
+                    start=h_sum(c, t)[1],
                     stop=False,
                 )
 
@@ -165,13 +176,10 @@ def tile_picked_mixhgspanfrac_none_p_kernel(
 
         def gather_members(k):
             j0, n = pieces[k]
-            g = ring.tile([P, PACK, MEMBERS * n], F32, name="members", bufs=3)
+            g = ring.tile([P, PACK, MEMBERS * n], F32, name="members", bufs=len(pieces))
             lst = n1_t[:, j0 // 4 : (j0 + n) // 4]
             for t in range(PACK):
-                if (k, t) == (0, 1):
-                    nc.vector.tensor_copy(g[:, t, :], y_win[t][:].indirect(lst))
-                else:
-                    nc.scalar.activation(g[:, t, :], y_win[t][:].indirect(lst), ACT.Copy)
+                nc.scalar.activation(g[:, t, :], y_win[t][:].indirect(lst), ACT.Copy)
             state["g", k] = g
 
         def pairs(k, op, name):
@@ -202,24 +210,27 @@ def tile_picked_mixhgspanfrac_none_p_kernel(
             for t in range(PACK):
                 rows = slice(P * t, P * (t + 1))
                 nc.tensor.matmul_mx(
-                    out=h_ps[c][:, t, :],
+                    out=h_sum(c, t)[0],
                     lhsT=w2_codes[:, rows].bitcast(FP8X4),
                     lhsT_scale=w2_scales[:, rows],
                     rhs=z_codes[:].bitcast(FP8X4),
                     rhs_scale=z_scales[:],
                     start=False,
-                    stop=(t == PACK - 1),
+                    stop=h_sum(c, t)[2],
                 )
             empty_h(c)
 
         def empty_h(c):
             cols = slice(CHUNK * c, CHUNK * (c + 1))
-            nc.scalar.copy(h_plain[:, :, cols], h_ps[c][:])
-            for t in range(PACK):
-                if c == CHUNKS - 1 and t < 2:
-                    nc.vector.tensor_copy(h_win[t][:, cols], h_plain[:, t, cols])
-                else:
+            if c < CHUNKS - 1:
+                nc.scalar.copy(h_plain[:, :, cols], h_ps[c][:])
+                for t in range(PACK):
                     nc.sync.dma_start(h_win[t][:, cols], h_plain[:, t, cols])
+                return
+            for u, copy in enumerate((nc.vector.tensor_copy, nc.scalar.copy)):
+                nc.scalar.copy(h_plain[:, 2 * u : 2 * u + 2, cols], h_last[u][:])
+                for t in (2 * u, 2 * u + 1):
+                    copy(h_win[t][:, cols], h_plain[:, t, cols])
 
         for c in range(CHUNKS):
             hashed_product(c)
@@ -261,7 +272,7 @@ def tile_picked_mixhgspanfrac_none_p_kernel(
             parts["q", t] = q
 
         def numerator(t):
-            n = keep.tile([P, S], F32, name="d2_%d" % t)
+            n = ring.tile([P, S], F32, name="d2")
             if ("a", t) in parts:
                 nc.vector.tensor_tensor(n[:], parts["a", t][:], h_plain[:, t, :], ALU.subtract)
             else:
@@ -280,8 +291,8 @@ def tile_picked_mixhgspanfrac_none_p_kernel(
         inverse(0)
         distance(1)
         inverse(1)
-        numerator(0)
         distance(2)
+        numerator(0)
         quotient(0, 1)
         fetch(1)
         distance(3)
@@ -289,7 +300,7 @@ def tile_picked_mixhgspanfrac_none_p_kernel(
         numerator(2)
         numerator(1)
         quotient(1, 1)
+        quotient(2, 1)
         inverse(3)
         numerator(3)
-        quotient(2, 1)
         quotient(3, 2)

@@ -49,6 +49,12 @@ def tile_picked_mixhgspanfrac_none_p_kernel(
                 raw[:].rearrange("p j (m t) -> p m j t", t=PACK),
             )
 
+        def deal_pairs(grouped, raw, m0, m1):
+            nc.vector.tensor_copy(
+                grouped[:].rearrange("p (u t m j) -> p u m j t", u=2, t=2, j=PACK)[:, :, m0:m1],
+                raw[:].rearrange("p j (m u t) -> p u m j t", u=2, t=2),
+            )
+
         def mx_tiles(name, width):
             codes = keep.tile([P, width], U32, name=name + "_codes", align_bytes=64)
             scales = keep.tile([P, width], U8, name=name + "_scales", align_bytes=64)
@@ -98,7 +104,7 @@ def tile_picked_mixhgspanfrac_none_p_kernel(
         w1_grouped = keep.tile([P, PACK * 512], BF16, name="w1_grouped", tag="w1_grouped", align_bytes=64)
         w1_codes, w1_scales = mx_tiles("w1", 512)
         deal(nc.scalar.copy, w1_grouped, w1_raw[0], 0, 64)
-        deal(nc.vector.tensor_copy, w1_grouped, w1_raw[1], 64, 128)
+        deal_pairs(w1_grouped, w1_raw[1], 64, 128)
         nc.vector.tensor_copy(xq_codes[:], xw[:].indirect(offs_t[:]))
         nc.vector.tensor_copy(xq_scales[:], xs[:].indirect(offs_t[:]))
         for u in range(2):
@@ -135,7 +141,7 @@ def tile_picked_mixhgspanfrac_none_p_kernel(
         for name, raw in (("w3", w3_raw), ("w2", w2_raw)):
             grouped = keep.tile([P, PACK * 512], BF16, name=name + "_grouped", align_bytes=64)
             if name == "w3":
-                deal(nc.vector.tensor_copy, grouped, raw, 0, P)
+                deal_pairs(grouped, raw, 0, P)
             else:
                 signs = sign[:].unsqueeze(1).unsqueeze(3).to_broadcast([P, P, PACK, PACK])
                 deal(lambda o, i: nc.vector.tensor_tensor(o, i, signs, ALU.mult), grouped, raw, 0, P)
@@ -184,13 +190,13 @@ def tile_picked_mixhgspanfrac_none_p_kernel(
 
         def pairs(k, op, name):
             g = state["g", k][:].rearrange("p t (j h e) -> p j t h e", h=2, e=2)
-            r = ring.tile([P, pieces[k][1], PACK, 2], F32, name=name)
-            nc.vector.tensor_tensor(r[:], g[:, :, :, 0, :], g[:, :, :, 1, :], op)
+            r = ring.tile([P, pieces[k][1], 2, PACK], F32, name=name)
+            nc.vector.tensor_tensor(r[:].rearrange("p j e t -> p j t e"), g[:, :, :, 0, :], g[:, :, :, 1, :], op)
             state[name, k] = r
 
         def fours(k, op, src, name):
             r = ring.tile([P, pieces[k][1], PACK], F32, name=name)
-            nc.vector.tensor_tensor(r[:], state[src, k][:, :, :, 0], state[src, k][:, :, :, 1], op)
+            nc.vector.tensor_tensor(r[:], state[src, k][:, :, 0, :], state[src, k][:, :, 1, :], op)
             state[name, k] = r
 
         def span(k):
@@ -224,8 +230,10 @@ def tile_picked_mixhgspanfrac_none_p_kernel(
             cols = slice(CHUNK * c, CHUNK * (c + 1))
             if c < CHUNKS - 1:
                 nc.scalar.copy(h_plain[:, :, cols], h_ps[c][:])
-                for t in range(PACK):
-                    nc.sync.dma_start(h_win[t][:, cols], h_plain[:, t, cols])
+                if c > 0:
+                    cols = slice(0 if c == 1 else CHUNK * c, CHUNK * (c + 1))
+                    for t in range(PACK):
+                        nc.sync.dma_start(h_win[t][:, cols], h_plain[:, t, cols])
                 return
             for u, copy in enumerate((nc.vector.tensor_copy, nc.scalar.copy)):
                 nc.scalar.copy(h_plain[:, 2 * u : 2 * u + 2, cols], h_last[u][:])
@@ -262,13 +270,15 @@ def tile_picked_mixhgspanfrac_none_p_kernel(
             nc.vector.tensor_tensor(d[:], h_win[t][:].indirect(n3_t[:]), h_plain[:, t, :], ALU.subtract)
             parts["d", t] = d
 
-        def inverse(t):
-            a = ring.tile([P, S], F32, name="absd")
-            nc.scalar.activation(a[:], parts["d", t][:], ACT.Abs)
-            r = ring.tile([P, S], F32, name="root")
-            nc.scalar.activation(r[:], a[:], ACT.Abs_reciprocal_sqrt, bias=0.5)
+        def inverse(t, pieces):
             q = keep.tile([P, S], F32, name="inv%d" % t)
-            nc.scalar.activation(q[:], r[:], ACT.Square)
+            for k in range(pieces):
+                x = slice(S // pieces * k, S // pieces * (k + 1))
+                a = ring.tile([P, S // pieces], F32, name="absd")
+                nc.scalar.activation(a[:], parts["d", t][:, x], ACT.Abs)
+                r = ring.tile([P, S // pieces], F32, name="root")
+                nc.scalar.activation(r[:], a[:], ACT.Abs_reciprocal_sqrt, bias=0.5)
+                nc.scalar.activation(q[:, x], r[:], ACT.Square)
             parts["q", t] = q
 
         def numerator(t):
@@ -288,19 +298,20 @@ def tile_picked_mixhgspanfrac_none_p_kernel(
 
         fetch(0)
         distance(0)
-        inverse(0)
+        inverse(0, 1)
         distance(1)
-        inverse(1)
+        inverse(1, 1)
         distance(2)
-        numerator(0)
-        quotient(0, 1)
         fetch(1)
         distance(3)
-        inverse(2)
-        numerator(2)
+        numerator(0)
+        quotient(0, 1)
+        inverse(2, 1)
         numerator(1)
         quotient(1, 1)
-        quotient(2, 1)
-        inverse(3)
+        fetch(2)
         numerator(3)
+        inverse(3, 2)
+        numerator(2)
+        quotient(2, 1)
         quotient(3, 2)

@@ -14,14 +14,21 @@ ACT = mybir.ActivationFunctionType
 
 P = 128
 PACK = 4
+D = P * PACK
 T = 2048
 S = 512
 MEMBERS = 4
+LANES = 16
+QUADRANT = 32
 CHUNK = 128
 CHUNKS = S // CHUNK
 SPARE = 32
 
-FLOPS = 3 * 2 * 512 * 512 * 512
+PIECES = [(CHUNK * c, CHUNK) for c in range(CHUNKS - 1)] + [(S - CHUNK, CHUNK // 2), (S - CHUNK // 2, CHUNK // 2)]
+
+FETCHED = [S, S, S // 2, 0]
+
+FLOPS = 3 * 2 * D * D * S
 
 
 def tile_picked_mixhgspanfrac_none_p_kernel(
@@ -34,25 +41,28 @@ def tile_picked_mixhgspanfrac_none_p_kernel(
         psum = ctx.enter_context(tc.psum_pool(name="psum", bufs=1))
 
         def load_list(src, name):
-            lst = keep.tile(list(src.shape), U16, name=name)
-            nc.sync.dma_start(lst[:], src)
-            return lst
+            entries = keep.tile(list(src.shape), U16, name=name)
+            nc.sync.dma_start(entries[:], src)
+            return entries
 
-        def load_weight(w, name, c0, c1):
-            raw = keep.tile([P, PACK, c1 - c0], F32, name=name, tag=name, align_bytes=64)
-            nc.sync.dma_start(raw[:], w.rearrange("(p j) c -> p j c", j=PACK)[:, :, c0:c1])
+        def load_weight(w, name, part, parts):
+            width = D // parts
+            raw = keep.tile([P, PACK, width], F32, name=name, align_bytes=64)
+            nc.sync.dma_start(raw[:], w.rearrange("(p s) c -> p s c", s=PACK)[:, :, width * part : width * (part + 1)])
             return raw
 
-        def deal(copy, grouped, raw, m0, m1):
-            copy(
-                grouped[:].rearrange("p (t m j) -> p m j t", t=PACK, j=PACK)[:, m0:m1],
-                raw[:].rearrange("p j (m t) -> p m j t", t=PACK),
+        def dealing_views(dealt, raw, part, parts):
+            m = slice(P // parts * part, P // parts * (part + 1))
+            return (
+                dealt[:].rearrange("p (t m s) -> p m s t", t=PACK, s=PACK)[:, m],
+                raw[:].rearrange("p s (m t) -> p m s t", t=PACK),
             )
 
-        def deal_pairs(grouped, raw, m0, m1):
+        def deal_on_vector(dealt, raw, part, parts):
+            m = slice(P // parts * part, P // parts * (part + 1))
             nc.vector.tensor_copy(
-                grouped[:].rearrange("p (u t m j) -> p u m j t", u=2, t=2, j=PACK)[:, :, m0:m1],
-                raw[:].rearrange("p j (m u t) -> p u m j t", u=2, t=2),
+                dealt[:].rearrange("p (u v m s) -> p u m s v", u=2, v=2, s=PACK)[:, :, m],
+                raw[:].rearrange("p s (m u v) -> p u m s v", u=2, v=2),
             )
 
         def mx_tiles(name, width):
@@ -60,35 +70,51 @@ def tile_picked_mixhgspanfrac_none_p_kernel(
             scales = keep.tile([P, width], U8, name=name + "_scales", align_bytes=64)
             return codes, scales
 
+        def quantize(mx, cols, values):
+            codes, scales = mx
+            nc.vector.quantize_mx(out=codes[:, cols].bitcast(FP8X4), scales=scales[:, cols], in_=values)
+
+        def product(acc, w_mx, t, x_mx, cols, start, stop):
+            rows = slice(P * t, P * (t + 1))
+            nc.tensor.matmul_mx(
+                out=acc,
+                lhsT=w_mx[0][:, rows].bitcast(FP8X4),
+                lhsT_scale=w_mx[1][:, rows],
+                rhs=x_mx[0][:, cols].bitcast(FP8X4),
+                rhs_scale=x_mx[1][:, cols],
+                start=start,
+                stop=stop,
+            )
+
         warm = keep.tile([P, 2], F32, name="warm")
         nc.vector.memset(warm[:, 0:1], 1.0)
         nc.scalar.activation(warm[:, 1:2], warm[:, 0:1], ACT.Abs_reciprocal_sqrt)
-        xs = keep.tile([P, T], U8, name="xs", align_bytes=64)
-        nc.vector.memset(xs[:].bitcast(I32), 0)
-        xs_runs = keep.tile([P, T], U8, name="xs_runs", align_bytes=64)
-        nc.vector.memset(xs_runs[:].bitcast(I32), 0)
-        scale_rows = x_scales[0].bitcast(I32)
+
         offs_t = load_list(offs, "offs_t")
         hz_t = load_list(hz, "hz_t")
-        n1_t = load_list(n1, "n1_t")
-        n2_t = load_list(n2, "n2_t")
-        n3_t = load_list(n3, "n3_t")
+        xs = keep.tile([P, T], U8, name="xs", align_bytes=64)
+        scale_rows = x_scales[0].bitcast(I32)
+        for q in range(P // QUADRANT):
+            nc.sync.dma_start(
+                xs[:].bitcast(I32)[QUADRANT * q : QUADRANT * (q + 1), :],
+                scale_rows[4 * q : 4 * (q + 1), :].partition_broadcast(QUADRANT // 4),
+            )
+        w1_raw = [load_weight(w1, "w1_raw%d" % half, half, 2) for half in range(2)]
+        xw = keep.tile([P, T], U32, name="xw", align_bytes=64)
+        nc.sync.dma_start(xw[:].bitcast(I32), x_words[0].rearrange("p n s -> p (n s)").bitcast(I32))
         gain = keep.tile([P, PACK], F32, name="gain")
         nc.sync.dma_start(gain[:], gn.rearrange("(p t) o -> p (t o)", t=PACK))
-        xw = keep.tile([P, T], U32, name="xw", align_bytes=64)
-        nc.sync.dma_start(xw[:].bitcast(I32), x_words[0].rearrange("p n t -> p (n t)").bitcast(I32))
-        for b in range(4):
-            nc.sync.dma_start(xs[:].bitcast(I32)[b:P:32, :], scale_rows[b:16:4, :])
-        w1_raw = [load_weight(w1, "w1_raw%d" % h, 256 * h, 256 * (h + 1)) for h in range(2)]
-        nc.sync.dma_start(xs_runs[:].bitcast(I32)[0:P:8, :], scale_rows)
-        w3_raw = load_weight(w3, "w3_raw", 0, 512)
-        w2_raw = load_weight(w2, "w2_raw", 0, 512)
+        n1_t = load_list(n1, "n1_t")
+        w2_raw = [load_weight(w2, "w2_raw%d" % half, half, 2) for half in range(2)]
+        w3_raw = load_weight(w3, "w3_raw", 0, 1)
+        n2_t = load_list(n2, "n2_t")
+        n3_t = load_list(n3, "n3_t")
 
         y_win = [keep.tile([P, S + SPARE], F32, name="y_win%d" % t) for t in range(PACK)]
         for t in range(PACK):
             nc.vector.memset(y_win[t][:, S:], 0.0)
-        xh_plane = keep.tile([P, S], U8, name="xh_plane", align_bytes=64)
-        nc.vector.memset(xh_plane[:].bitcast(I32), 0)
+        xh_scales = keep.tile([P, S], U8, name="xh_scales", align_bytes=64)
+        nc.vector.memset(xh_scales[:].bitcast(I32), 0)
         h_win = [keep.tile([P, 2 * S], F32, name="h_win%d" % t) for t in range(PACK)]
         for t in range(PACK):
             nc.vector.memset(h_win[t][:, S:], 0.0)
@@ -100,218 +126,181 @@ def tile_picked_mixhgspanfrac_none_p_kernel(
         size = keep.tile([P, PACK], F32, name="size")
         nc.vector.tensor_tensor(size[:], gain[:], sign[:], ALU.mult)
 
-        xq_codes, xq_scales = mx_tiles("xq", S)
-        w1_grouped = keep.tile([P, PACK * 512], BF16, name="w1_grouped", tag="w1_grouped", align_bytes=64)
-        w1_codes, w1_scales = mx_tiles("w1", 512)
-        deal(nc.scalar.copy, w1_grouped, w1_raw[0], 0, 64)
-        deal_pairs(w1_grouped, w1_raw[1], 64, 128)
-        nc.vector.tensor_copy(xq_codes[:], xw[:].indirect(offs_t[:]))
-        nc.vector.tensor_copy(xq_scales[:], xs[:].indirect(offs_t[:]))
+        xq_mx = mx_tiles("xq", S)
+        w1_dealt = keep.tile([P, PACK * D], BF16, name="w1_dealt", align_bytes=64)
+        w1_mx = mx_tiles("w1", D)
+        nc.scalar.copy(*dealing_views(w1_dealt, w1_raw[0], 0, 2))
+        deal_on_vector(w1_dealt, w1_raw[1], 1, 2)
+        nc.vector.tensor_copy(xq_mx[0][:], xw[:].indirect(offs_t[:]))
+        nc.vector.tensor_copy(xq_mx[1][:], xs[:].indirect(offs_t[:]))
         for u in range(2):
-            cols = slice(256 * u, 256 * (u + 1))
-            nc.vector.quantize_mx(
-                out=w1_codes[:, cols].bitcast(FP8X4),
-                scales=w1_scales[:, cols],
-                in_=w1_grouped[:, 1024 * u : 1024 * (u + 1)],
+            quantize(w1_mx, slice(2 * P * u, 2 * P * (u + 1)), w1_dealt[:, 2 * D * u : 2 * D * (u + 1)])
+
+        xh_bytes = keep.tile([P, S], U8, name="xh_bytes", align_bytes=64)
+        xh_codes = keep.tile([P, S], U32, name="xh_codes", align_bytes=64)
+        xh_mx = (xh_codes, xh_scales)
+        nc.vector.tensor_copy(xh_bytes[:], xs[:].indirect(hz_t[:]))
+        for row in range(4):
+            found = row if row < 2 else LANES + row
+            nc.sync.dma_start(
+                xh_scales[:].bitcast(I32)[row:P:QUADRANT, :], xh_bytes[:].bitcast(I32)[found:P:QUADRANT, :]
             )
-        xh_bytes = keep.tile([P, S], U8, name="xh_bytes", tag="w1_raw1", align_bytes=64)
-        xh_codes = keep.tile([P, S], U32, name="xh_codes", tag="w1_grouped", align_bytes=64)
-        nc.vector.tensor_copy(xh_bytes[:], xs_runs[:].indirect(hz_t[:]))
-        for b in range(4):
-            nc.sync.dma_start(xh_plane[:].bitcast(I32)[b:P:32, :], xh_bytes[:].bitcast(I32)[8 * b : P : 32, :])
+
         for t in range(PACK):
             y_ps = psum.tile([P, S], F32, name="y_ps%d" % t, tag="y_ps%d" % t)
-            cols = slice(P * t, P * (t + 1))
-            nc.tensor.matmul_mx(
-                out=y_ps[:],
-                lhsT=w1_codes[:, cols].bitcast(FP8X4),
-                lhsT_scale=w1_scales[:, cols],
-                rhs=xq_codes[:].bitcast(FP8X4),
-                rhs_scale=xq_scales[:],
-                start=True,
-                stop=True,
-            )
+            product(y_ps[:], w1_mx, t, xq_mx, slice(0, S), True, True)
             if t % 2:
                 nc.vector.tensor_scalar(y_win[t][:, :S], y_ps[:], size[:, t : t + 1], None, ALU.mult)
             else:
                 nc.scalar.activation(y_win[t][:, :S], y_ps[:], ACT.Copy, scale=size[:, t : t + 1])
 
         nc.vector.tensor_copy(xh_codes[:], xw[:].indirect(hz_t[:]))
-        w_mx = {}
-        for name, raw in (("w3", w3_raw), ("w2", w2_raw)):
-            grouped = keep.tile([P, PACK * 512], BF16, name=name + "_grouped", align_bytes=64)
-            if name == "w3":
-                deal_pairs(grouped, raw, 0, P)
-            else:
-                signs = sign[:].unsqueeze(1).unsqueeze(3).to_broadcast([P, P, PACK, PACK])
-                deal(lambda o, i: nc.vector.tensor_tensor(o, i, signs, ALU.mult), grouped, raw, 0, P)
-            w_mx[name] = (grouped,) + mx_tiles(name, 512)
-        for name in ("w3", "w2"):
-            grouped, codes, scales = w_mx[name]
-            nc.vector.quantize_mx(out=codes[:].bitcast(FP8X4), scales=scales[:], in_=grouped[:])
-        w3_codes, w3_scales = w_mx["w3"][1:]
-        w2_codes, w2_scales = w_mx["w2"][1:]
+        w2_dealt = keep.tile([P, PACK * D], BF16, name="w2_dealt", align_bytes=64)
+        row_signs = sign[:].unsqueeze(1).unsqueeze(3).to_broadcast([P, P // 2, PACK, PACK])
+        for half in range(2):
+            nc.vector.tensor_tensor(*dealing_views(w2_dealt, w2_raw[half], half, 2), row_signs, ALU.mult)
+        w2_mx = mx_tiles("w2", D)
+        quantize(w2_mx, slice(0, D), w2_dealt[:])
+        w3_dealt = keep.tile([P, PACK * D], BF16, name="w3_dealt", align_bytes=64)
+        deal_on_vector(w3_dealt, w3_raw, 0, 1)
+        w3_mx = mx_tiles("w3", D)
+        quantize(w3_mx, slice(0, D), w3_dealt[:])
 
         h_ps = [psum.tile([P, PACK, CHUNK], F32, name="h_ps%d" % c) for c in range(CHUNKS - 1)]
-        h_last = [psum.tile([P, 2, CHUNK], F32, name="h_last%d" % u, tag="y_ps%d" % u) for u in range(2)]
+        h_last = [psum.tile([P, CHUNK], F32, name="h_last%d" % t, tag="y_ps%d" % t) for t in range(PACK)]
 
         def h_sum(c, t):
             if c < CHUNKS - 1:
                 return h_ps[c][:, t, :], t == 0, t == PACK - 1
-            return h_last[t // 2][:, t % 2, :], t % 2 == 0, t % 2 == 1
+            return h_last[t][:], True, True
 
         h_plain = keep.tile([P, PACK, S], F32, name="h_plain")
-
-        def hashed_product(c):
-            cols = slice(CHUNK * c, CHUNK * (c + 1))
-            for t in range(PACK):
-                rows = slice(P * t, P * (t + 1))
-                nc.tensor.matmul_mx(
-                    out=h_sum(c, t)[0],
-                    lhsT=w3_codes[:, rows].bitcast(FP8X4),
-                    lhsT_scale=w3_scales[:, rows],
-                    rhs=xh_codes[:, cols].bitcast(FP8X4),
-                    rhs_scale=xh_plane[:, cols],
-                    start=h_sum(c, t)[1],
-                    stop=False,
-                )
-
-        state = {}
         z_mx = [mx_tiles("z%d" % c, CHUNK) for c in range(CHUNKS)]
-        pieces = [(CHUNK * c, CHUNK) for c in range(CHUNKS - 1)] + [(S - CHUNK, CHUNK // 2), (S - CHUNK // 2, CHUNK // 2)]
+        members, pair, four, z = {}, {}, {}, {}
 
         def gather_members(k):
-            j0, n = pieces[k]
-            g = ring.tile([P, PACK, MEMBERS * n], F32, name="members", bufs=len(pieces))
-            lst = n1_t[:, j0 // 4 : (j0 + n) // 4]
+            j0, width = PIECES[k]
+            members[k] = ring.tile([P, PACK, MEMBERS * width], F32, name="members", bufs=len(PIECES))
+            entries = n1_t[:, MEMBERS * j0 // LANES : MEMBERS * (j0 + width) // LANES]
             for t in range(PACK):
-                nc.scalar.activation(g[:, t, :], y_win[t][:].indirect(lst), ACT.Copy)
-            state["g", k] = g
+                nc.scalar.activation(members[k][:, t, :], y_win[t][:].indirect(entries), ACT.Copy)
 
-        def pairs(k, op, name):
-            g = state["g", k][:].rearrange("p t (j h e) -> p j t h e", h=2, e=2)
-            r = ring.tile([P, pieces[k][1], 2, PACK], F32, name=name)
-            nc.vector.tensor_tensor(r[:].rearrange("p j e t -> p j t e"), g[:, :, :, 0, :], g[:, :, :, 1, :], op)
-            state[name, k] = r
+        def of_pairs(k, op, name):
+            both = members[k][:].rearrange("p t (j h e) -> p j t h e", h=2, e=2)
+            pair[k, op] = ring.tile([P, PIECES[k][1], 2, PACK], F32, name=name)
+            nc.vector.tensor_tensor(
+                pair[k, op][:].rearrange("p j e t -> p j t e"), both[:, :, :, 0, :], both[:, :, :, 1, :], op
+            )
 
-        def fours(k, op, src, name):
-            r = ring.tile([P, pieces[k][1], PACK], F32, name=name)
-            nc.vector.tensor_tensor(r[:], state[src, k][:, :, 0, :], state[src, k][:, :, 1, :], op)
-            state[name, k] = r
+        def of_four(k, op, name):
+            four[k, op] = ring.tile([P, PIECES[k][1], PACK], F32, name=name)
+            nc.vector.tensor_tensor(four[k, op][:], pair[k, op][:, :, 0, :], pair[k, op][:, :, 1, :], op)
 
         def span(k):
-            z = ring.tile([P, pieces[k][1] * PACK], BF16, name="z", align_bytes=64)
-            flat = lambda name: state[name, k][:].rearrange("p j t -> p (j t)")
-            nc.vector.scalar_tensor_tensor(z[:], flat("mn"), -0.5, flat("mx"), ALU.mult, ALU.add)
-            state["z", k] = z
+            z[k] = ring.tile([P, PIECES[k][1] * PACK], BF16, name="z", align_bytes=64)
+            low, high = [four[k, op][:].rearrange("p j t -> p (j t)") for op in (ALU.min, ALU.max)]
+            nc.vector.scalar_tensor_tensor(z[k][:], low, -0.5, high, ALU.mult, ALU.add)
 
         def second_product(k):
-            j0, n = pieces[k]
+            j0, width = PIECES[k]
             c = j0 // CHUNK
-            z_codes, z_scales = z_mx[c]
-            x = slice(j0 % CHUNK, j0 % CHUNK + n)
-            nc.vector.quantize_mx(out=z_codes[:, x].bitcast(FP8X4), scales=z_scales[:, x], in_=state["z", k][:])
-            if (j0 + n) % CHUNK:
-                return
-            for t in range(PACK):
-                rows = slice(P * t, P * (t + 1))
-                nc.tensor.matmul_mx(
-                    out=h_sum(c, t)[0],
-                    lhsT=w2_codes[:, rows].bitcast(FP8X4),
-                    lhsT_scale=w2_scales[:, rows],
-                    rhs=z_codes[:].bitcast(FP8X4),
-                    rhs_scale=z_scales[:],
-                    start=False,
-                    stop=h_sum(c, t)[2],
-                )
-            empty_h(c)
+            quantize(z_mx[c], slice(j0 % CHUNK, j0 % CHUNK + width), z[k][:])
+            if (j0 + width) % CHUNK == 0:
+                for t in range(PACK):
+                    acc, first, last = h_sum(c, t)
+                    product(acc, w2_mx, t, z_mx[c], slice(0, CHUNK), False, last)
+                empty_h(c)
 
         def empty_h(c):
             cols = slice(CHUNK * c, CHUNK * (c + 1))
             if c < CHUNKS - 1:
                 nc.scalar.copy(h_plain[:, :, cols], h_ps[c][:])
                 if c > 0:
-                    cols = slice(0 if c == 1 else CHUNK * c, CHUNK * (c + 1))
+                    moved = slice(0 if c == 1 else CHUNK * c, CHUNK * (c + 1))
                     for t in range(PACK):
-                        nc.sync.dma_start(h_win[t][:, cols], h_plain[:, t, cols])
+                        nc.sync.dma_start(h_win[t][:, moved], h_plain[:, t, moved])
                 return
-            for u, copy in enumerate((nc.vector.tensor_copy, nc.scalar.copy)):
-                nc.scalar.copy(h_plain[:, 2 * u : 2 * u + 2, cols], h_last[u][:])
-                for t in (2 * u, 2 * u + 1):
-                    copy(h_win[t][:, cols], h_plain[:, t, cols])
+            for t in range(PACK):
+                copy = nc.scalar.copy if t else nc.vector.tensor_copy
+                copy(h_plain[:, t, cols], h_last[t][:])
+                if t < PACK - 1:
+                    copy(h_win[t][:, cols], h_last[t][:])
+                else:
+                    nc.sync.dma_start(h_win[t][:, cols], h_plain[:, t, cols])
 
         for c in range(CHUNKS):
-            hashed_product(c)
-        for k in range(len(pieces) + 1):
-            more = k < len(pieces)
+            for t in range(PACK):
+                acc, first, last = h_sum(c, t)
+                product(acc, w3_mx, t, xh_mx, slice(CHUNK * c, CHUNK * (c + 1)), first, False)
+
+        for k in range(len(PIECES) + 1):
+            more = k < len(PIECES)
             if more:
                 gather_members(k)
-                pairs(k, ALU.max, "mx2")
+                of_pairs(k, ALU.max, "max_pair")
             if k > 0:
                 span(k - 1)
             if more:
-                pairs(k, ALU.min, "mn2")
+                of_pairs(k, ALU.min, "min_pair")
             if k > 0:
                 second_product(k - 1)
             if more:
-                fours(k, ALU.max, "mx2", "mx")
-                fours(k, ALU.min, "mn2", "mn")
+                of_four(k, ALU.max, "max_four")
+                of_four(k, ALU.min, "min_four")
 
         out_rows = out.rearrange("(p t) c -> p t c", t=PACK)
-        parts = {}
+        fetched, distance, inverse, minus_top = {}, {}, {}, {}
 
         def fetch(t):
-            a = keep.tile([P, S], F32, name="fetched%d" % t)
-            nc.scalar.activation(a[:], h_win[t][:].indirect(n2_t[:]), ACT.Copy)
-            parts["a", t] = a
+            fetched[t] = keep.tile([P, FETCHED[t]], F32, name="fetched%d" % t)
+            nc.scalar.activation(fetched[t][:], h_win[t][:].indirect(n2_t[:, : FETCHED[t] // LANES]), ACT.Copy)
 
-        def distance(t):
-            d = keep.tile([P, S], F32, name="d3_%d" % t)
-            nc.vector.tensor_tensor(d[:], h_win[t][:].indirect(n3_t[:]), h_plain[:, t, :], ALU.subtract)
-            parts["d", t] = d
+        def measure(t):
+            distance[t] = keep.tile([P, S], F32, name="distance%d" % t)
+            nc.vector.tensor_tensor(distance[t][:], h_win[t][:].indirect(n3_t[:]), h_plain[:, t, :], ALU.subtract)
 
-        def inverse(t, pieces):
-            q = keep.tile([P, S], F32, name="inv%d" % t)
-            for k in range(pieces):
-                x = slice(S // pieces * k, S // pieces * (k + 1))
-                a = ring.tile([P, S // pieces], F32, name="absd")
-                nc.scalar.activation(a[:], parts["d", t][:, x], ACT.Abs)
-                r = ring.tile([P, S // pieces], F32, name="root")
-                nc.scalar.activation(r[:], a[:], ACT.Abs_reciprocal_sqrt, bias=0.5)
-                nc.scalar.activation(q[:, x], r[:], ACT.Square)
-            parts["q", t] = q
+        def invert(t):
+            inverse[t] = keep.tile([P, S], F32, name="inverse%d" % t)
+            length = ring.tile([P, S], F32, name="length")
+            nc.scalar.activation(length[:], distance[t][:], ACT.Abs)
+            root = ring.tile([P, S], F32, name="root")
+            nc.scalar.activation(root[:], length[:], ACT.Abs_reciprocal_sqrt, bias=0.5)
+            nc.scalar.activation(inverse[t][:], root[:], ACT.Square)
 
-        def numerator(t):
-            n = ring.tile([P, S], F32, name="d2")
-            if ("a", t) in parts:
-                nc.vector.tensor_tensor(n[:], parts["a", t][:], h_plain[:, t, :], ALU.subtract)
-            else:
-                nc.vector.tensor_tensor(n[:], h_win[t][:].indirect(n2_t[:]), h_plain[:, t, :], ALU.subtract)
-            parts["n", t] = n
+        def subtract(t):
+            minus_top[t] = ring.tile([P, S], F32, name="minus_top")
+            width = FETCHED[t]
+            if width < S:
+                looked_up = h_win[t][:].indirect(n2_t[:, width // LANES :])
+                nc.vector.tensor_tensor(minus_top[t][:, width:], looked_up, h_plain[:, t, width:], ALU.subtract)
+            if width > 0:
+                nc.vector.tensor_tensor(minus_top[t][:, :width], fetched[t][:], h_plain[:, t, :width], ALU.subtract)
 
-        def quotient(t, pieces):
-            o = keep.tile([P, S], F32, name="o%d" % t)
-            for k in range(pieces):
-                x = slice(S // pieces * k, S // pieces * (k + 1))
-                nc.vector.scalar_tensor_tensor(o[:, x], parts["n", t][:, x], -1.0, parts["q", t][:, x], ALU.mult, ALU.mult)
-                nc.sync.dma_start(out_rows[:, t, x], o[:, x])
+        def divide(t, parts):
+            result = keep.tile([P, S], F32, name="result%d" % t)
+            for part in range(parts):
+                cols = slice(S // parts * part, S // parts * (part + 1))
+                nc.vector.scalar_tensor_tensor(
+                    result[:, cols], minus_top[t][:, cols], -1.0, inverse[t][:, cols], ALU.mult, ALU.mult
+                )
+                nc.sync.dma_start(out_rows[:, t, cols], result[:, cols])
 
         fetch(0)
-        distance(0)
-        inverse(0, 1)
-        distance(1)
-        inverse(1, 1)
-        distance(2)
+        measure(0)
+        invert(0)
+        measure(1)
+        invert(1)
+        measure(2)
+        subtract(0)
+        divide(0, 1)
         fetch(1)
-        distance(3)
-        numerator(0)
-        quotient(0, 1)
-        inverse(2, 1)
-        numerator(1)
-        quotient(1, 1)
         fetch(2)
-        numerator(3)
-        inverse(3, 2)
-        numerator(2)
-        quotient(2, 1)
-        quotient(3, 2)
+        measure(3)
+        invert(2)
+        subtract(2)
+        subtract(1)
+        divide(1, 1)
+        divide(2, 1)
+        invert(3)
+        subtract(3)
+        divide(3, 2)

from contextlib import ExitStack

import concourse.mybir as mybir

F32 = mybir.dt.float32
BF16 = mybir.dt.bfloat16
I32 = mybir.dt.int32
U32 = mybir.dt.uint32
U16 = mybir.dt.uint16
U8 = mybir.dt.uint8
FP8X4 = mybir.dt.float8_e4m3fn_x4
ALU = mybir.AluOpType
ACT = mybir.ActivationFunctionType

P = 128
PACK = 4
D = P * PACK
T = 2048
S = 512
MEMBERS = 4
LANES = 16
QUADRANT = 32
CHUNK = 128
CHUNKS = S // CHUNK
SPARE = 32

PIECES = [(CHUNK * c, CHUNK) for c in range(CHUNKS - 1)] + [(S - CHUNK, CHUNK // 2), (S - CHUNK // 2, CHUNK // 2)]

FETCHED = [S, S, S // 2, 0]

FLOPS = 3 * 2 * D * D * S


def tile_picked_mixhgspanfrac_none_p_kernel(
    tc, x_words, x_scales, w1, gn, w2, w3, offs, n1, hz, n2, n3, out
):
    nc = tc.nc
    with ExitStack() as ctx:
        keep = ctx.enter_context(tc.tile_pool(name="keep", bufs=1))
        ring = ctx.enter_context(tc.tile_pool(name="ring", bufs=2))
        psum = ctx.enter_context(tc.psum_pool(name="psum", bufs=1))

        def load_list(src, name):
            entries = keep.tile(list(src.shape), U16, name=name)
            nc.sync.dma_start(entries[:], src)
            return entries

        def load_weight(w, name, part, parts):
            width = D // parts
            raw = keep.tile([P, PACK, width], F32, name=name, align_bytes=64)
            nc.sync.dma_start(raw[:], w.rearrange("(p s) c -> p s c", s=PACK)[:, :, width * part : width * (part + 1)])
            return raw

        def dealing_views(dealt, raw, part, parts):
            m = slice(P // parts * part, P // parts * (part + 1))
            return (
                dealt[:].rearrange("p (t m s) -> p m s t", t=PACK, s=PACK)[:, m],
                raw[:].rearrange("p s (m t) -> p m s t", t=PACK),
            )

        def deal_on_vector(dealt, raw, part, parts):
            m = slice(P // parts * part, P // parts * (part + 1))
            nc.vector.tensor_copy(
                dealt[:].rearrange("p (u v m s) -> p u m s v", u=2, v=2, s=PACK)[:, :, m],
                raw[:].rearrange("p s (m u v) -> p u m s v", u=2, v=2),
            )

        def mx_tiles(name, width):
            codes = keep.tile([P, width], U32, name=name + "_codes", align_bytes=64)
            scales = keep.tile([P, width], U8, name=name + "_scales", align_bytes=64)
            return codes, scales

        def quantize(mx, cols, values):
            codes, scales = mx
            nc.vector.quantize_mx(out=codes[:, cols].bitcast(FP8X4), scales=scales[:, cols], in_=values)

        def product(acc, w_mx, t, x_mx, cols, start, stop):
            rows = slice(P * t, P * (t + 1))
            nc.tensor.matmul_mx(
                out=acc,
                lhsT=w_mx[0][:, rows].bitcast(FP8X4),
                lhsT_scale=w_mx[1][:, rows],
                rhs=x_mx[0][:, cols].bitcast(FP8X4),
                rhs_scale=x_mx[1][:, cols],
                start=start,
                stop=stop,
            )

        warm = keep.tile([P, 2], F32, name="warm")
        nc.vector.memset(warm[:, 0:1], 1.0)
        nc.scalar.activation(warm[:, 1:2], warm[:, 0:1], ACT.Abs_reciprocal_sqrt)

        offs_t = load_list(offs, "offs_t")
        hz_t = load_list(hz, "hz_t")
        xs = keep.tile([P, T], U8, name="xs", align_bytes=64)
        scale_rows = x_scales[0].bitcast(I32)
        for q in range(P // QUADRANT):
            nc.sync.dma_start(
                xs[:].bitcast(I32)[QUADRANT * q : QUADRANT * (q + 1), :],
                scale_rows[4 * q : 4 * (q + 1), :].partition_broadcast(QUADRANT // 4),
            )
        w1_raw = [load_weight(w1, "w1_raw%d" % half, half, 2) for half in range(2)]
        xw = keep.tile([P, T], U32, name="xw", align_bytes=64)
        nc.sync.dma_start(xw[:].bitcast(I32), x_words[0].rearrange("p n s -> p (n s)").bitcast(I32))
        gain = keep.tile([P, PACK], F32, name="gain")
        nc.sync.dma_start(gain[:], gn.rearrange("(p t) o -> p (t o)", t=PACK))
        n1_t = load_list(n1, "n1_t")
        w2_raw = [load_weight(w2, "w2_raw%d" % half, half, 2) for half in range(2)]
        w3_raw = load_weight(w3, "w3_raw", 0, 1)
        n2_t = load_list(n2, "n2_t")
        n3_t = load_list(n3, "n3_t")

        y_win = [keep.tile([P, S + SPARE], F32, name="y_win%d" % t) for t in range(PACK)]
        for t in range(PACK):
            nc.vector.memset(y_win[t][:, S:], 0.0)
        xh_scales = keep.tile([P, S], U8, name="xh_scales", align_bytes=64)
        nc.vector.memset(xh_scales[:].bitcast(I32), 0)
        h_win = [keep.tile([P, 2 * S], F32, name="h_win%d" % t) for t in range(PACK)]
        for t in range(PACK):
            nc.vector.memset(h_win[t][:, S:], 0.0)

        step = keep.tile([P, PACK], F32, name="step")
        nc.vector.tensor_scalar(step[:], gain[:], 0.0, 2.0, ALU.is_ge, ALU.mult)
        sign = keep.tile([P, PACK], F32, name="sign")
        nc.vector.tensor_scalar(sign[:], step[:], 1.0, None, ALU.subtract)
        size = keep.tile([P, PACK], F32, name="size")
        nc.vector.tensor_tensor(size[:], gain[:], sign[:], ALU.mult)

        xq_mx = mx_tiles("xq", S)
        w1_dealt = keep.tile([P, PACK * D], BF16, name="w1_dealt", align_bytes=64)
        w1_mx = mx_tiles("w1", D)
        nc.scalar.copy(*dealing_views(w1_dealt, w1_raw[0], 0, 2))
        deal_on_vector(w1_dealt, w1_raw[1], 1, 2)
        nc.vector.tensor_copy(xq_mx[0][:], xw[:].indirect(offs_t[:]))
        nc.vector.tensor_copy(xq_mx[1][:], xs[:].indirect(offs_t[:]))
        for u in range(2):
            quantize(w1_mx, slice(2 * P * u, 2 * P * (u + 1)), w1_dealt[:, 2 * D * u : 2 * D * (u + 1)])

        xh_bytes = keep.tile([P, S], U8, name="xh_bytes", align_bytes=64)
        xh_codes = keep.tile([P, S], U32, name="xh_codes", align_bytes=64)
        xh_mx = (xh_codes, xh_scales)
        nc.vector.tensor_copy(xh_bytes[:], xs[:].indirect(hz_t[:]))
        for row in range(4):
            found = row if row < 2 else LANES + row
            nc.sync.dma_start(
                xh_scales[:].bitcast(I32)[row:P:QUADRANT, :], xh_bytes[:].bitcast(I32)[found:P:QUADRANT, :]
            )

        for t in range(PACK):
            y_ps = psum.tile([P, S], F32, name="y_ps%d" % t, tag="y_ps%d" % t)
            product(y_ps[:], w1_mx, t, xq_mx, slice(0, S), True, True)
            if t % 2:
                nc.vector.tensor_scalar(y_win[t][:, :S], y_ps[:], size[:, t : t + 1], None, ALU.mult)
            else:
                nc.scalar.activation(y_win[t][:, :S], y_ps[:], ACT.Copy, scale=size[:, t : t + 1])

        nc.vector.tensor_copy(xh_codes[:], xw[:].indirect(hz_t[:]))
        w2_dealt = keep.tile([P, PACK * D], BF16, name="w2_dealt", align_bytes=64)
        row_signs = sign[:].unsqueeze(1).unsqueeze(3).to_broadcast([P, P // 2, PACK, PACK])
        for half in range(2):
            nc.vector.tensor_tensor(*dealing_views(w2_dealt, w2_raw[half], half, 2), row_signs, ALU.mult)
        w2_mx = mx_tiles("w2", D)
        quantize(w2_mx, slice(0, D), w2_dealt[:])
        w3_dealt = keep.tile([P, PACK * D], BF16, name="w3_dealt", align_bytes=64)
        deal_on_vector(w3_dealt, w3_raw, 0, 1)
        w3_mx = mx_tiles("w3", D)
        quantize(w3_mx, slice(0, D), w3_dealt[:])

        h_ps = [psum.tile([P, PACK, CHUNK], F32, name="h_ps%d" % c) for c in range(CHUNKS - 1)]
        h_last = [psum.tile([P, CHUNK], F32, name="h_last%d" % t, tag="y_ps%d" % t) for t in range(PACK)]

        def h_sum(c, t):
            if c < CHUNKS - 1:
                return h_ps[c][:, t, :], t == 0, t == PACK - 1
            return h_last[t][:], True, True

        h_plain = keep.tile([P, PACK, S], F32, name="h_plain")
        z_mx = [mx_tiles("z%d" % c, CHUNK) for c in range(CHUNKS)]
        members, pair, four, z = {}, {}, {}, {}

        def gather_members(k):
            j0, width = PIECES[k]
            members[k] = ring.tile([P, PACK, MEMBERS * width], F32, name="members", bufs=len(PIECES))
            entries = n1_t[:, MEMBERS * j0 // LANES : MEMBERS * (j0 + width) // LANES]
            for t in range(PACK):
                nc.scalar.activation(members[k][:, t, :], y_win[t][:].indirect(entries), ACT.Copy)

        def of_pairs(k, op, name):
            both = members[k][:].rearrange("p t (j h e) -> p j t h e", h=2, e=2)
            pair[k, op] = ring.tile([P, PIECES[k][1], 2, PACK], F32, name=name)
            nc.vector.tensor_tensor(
                pair[k, op][:].rearrange("p j e t -> p j t e"), both[:, :, :, 0, :], both[:, :, :, 1, :], op
            )

        def of_four(k, op, name):
            four[k, op] = ring.tile([P, PIECES[k][1], PACK], F32, name=name)
            nc.vector.tensor_tensor(four[k, op][:], pair[k, op][:, :, 0, :], pair[k, op][:, :, 1, :], op)

        def span(k):
            z[k] = ring.tile([P, PIECES[k][1] * PACK], BF16, name="z", align_bytes=64)
            low, high = [four[k, op][:].rearrange("p j t -> p (j t)") for op in (ALU.min, ALU.max)]
            nc.vector.scalar_tensor_tensor(z[k][:], low, -0.5, high, ALU.mult, ALU.add)

        def second_product(k):
            j0, width = PIECES[k]
            c = j0 // CHUNK
            quantize(z_mx[c], slice(j0 % CHUNK, j0 % CHUNK + width), z[k][:])
            if (j0 + width) % CHUNK == 0:
                for t in range(PACK):
                    acc, first, last = h_sum(c, t)
                    product(acc, w2_mx, t, z_mx[c], slice(0, CHUNK), False, last)
                empty_h(c)

        def empty_h(c):
            cols = slice(CHUNK * c, CHUNK * (c + 1))
            if c < CHUNKS - 1:
                nc.scalar.copy(h_plain[:, :, cols], h_ps[c][:])
                if c > 0:
                    moved = slice(0 if c == 1 else CHUNK * c, CHUNK * (c + 1))
                    for t in range(PACK):
                        nc.sync.dma_start(h_win[t][:, moved], h_plain[:, t, moved])
                return
            for t in range(PACK):
                copy = nc.scalar.copy if t else nc.vector.tensor_copy
                copy(h_plain[:, t, cols], h_last[t][:])
                if t < PACK - 1:
                    copy(h_win[t][:, cols], h_last[t][:])
                else:
                    nc.sync.dma_start(h_win[t][:, cols], h_plain[:, t, cols])

        for c in range(CHUNKS):
            for t in range(PACK):
                acc, first, last = h_sum(c, t)
                product(acc, w3_mx, t, xh_mx, slice(CHUNK * c, CHUNK * (c + 1)), first, False)

        for k in range(len(PIECES) + 1):
            more = k < len(PIECES)
            if more:
                gather_members(k)
                of_pairs(k, ALU.max, "max_pair")
            if k > 0:
                span(k - 1)
            if more:
                of_pairs(k, ALU.min, "min_pair")
            if k > 0:
                second_product(k - 1)
            if more:
                of_four(k, ALU.max, "max_four")
                of_four(k, ALU.min, "min_four")

        out_rows = out.rearrange("(p t) c -> p t c", t=PACK)
        fetched, distance, inverse, minus_top = {}, {}, {}, {}

        def fetch(t):
            fetched[t] = keep.tile([P, FETCHED[t]], F32, name="fetched%d" % t)
            nc.scalar.activation(fetched[t][:], h_win[t][:].indirect(n2_t[:, : FETCHED[t] // LANES]), ACT.Copy)

        def measure(t):
            distance[t] = keep.tile([P, S], F32, name="distance%d" % t)
            nc.vector.tensor_tensor(distance[t][:], h_win[t][:].indirect(n3_t[:]), h_plain[:, t, :], ALU.subtract)

        def invert(t):
            inverse[t] = keep.tile([P, S], F32, name="inverse%d" % t)
            length = ring.tile([P, S], F32, name="length")
            nc.scalar.activation(length[:], distance[t][:], ACT.Abs)
            root = ring.tile([P, S], F32, name="root")
            nc.scalar.activation(root[:], length[:], ACT.Abs_reciprocal_sqrt, bias=0.5)
            nc.scalar.activation(inverse[t][:], root[:], ACT.Square)

        def subtract(t):
            minus_top[t] = ring.tile([P, S], F32, name="minus_top")
            width = FETCHED[t]
            if width < S:
                looked_up = h_win[t][:].indirect(n2_t[:, width // LANES :])
                nc.vector.tensor_tensor(minus_top[t][:, width:], looked_up, h_plain[:, t, width:], ALU.subtract)
            if width > 0:
                nc.vector.tensor_tensor(minus_top[t][:, :width], fetched[t][:], h_plain[:, t, :width], ALU.subtract)

        def divide(t, parts):
            result = keep.tile([P, S], F32, name="result%d" % t)
            for part in range(parts):
                cols = slice(S // parts * part, S // parts * (part + 1))
                nc.vector.scalar_tensor_tensor(
                    result[:, cols], minus_top[t][:, cols], -1.0, inverse[t][:, cols], ALU.mult, ALU.mult
                )
                nc.sync.dma_start(out_rows[:, t, cols], result[:, cols])

        fetch(0)
        measure(0)
        invert(0)
        measure(1)
        invert(1)
        measure(2)
        subtract(0)
        divide(0, 1)
        fetch(1)
        fetch(2)
        measure(3)
        invert(2)
        subtract(2)
        subtract(1)
        divide(1, 1)
        divide(2, 1)
        invert(3)
        subtract(3)
        divide(3, 2)
